import numpy as np
CORES = [115,116,123,124]
N = 4
def setup_inputs(rng):
    return {"x": rng.standard_normal((N, 128, 2048), dtype=np.float32)}
def reference(x):
    s = x.sum(axis=0, dtype=np.float64).astype(x.dtype)
    b = 2048 // N
    return {"y": np.stack([s[:, r * b:(r + 1) * b] for r in range(N)])}

from concourse.bass import DstId, RemoteDMATransfer
from concourse.mybir import AluOpType

ROWS = 128
N = 4
B = 2048 // N
K = 2
W = B // K
RK = ROWS // K

SCRATCH = {
    "st": ("dram", [2 * K, ROWS, W], "float32"),
    "sp": ("dram", [ROWS, B], "float32"),
    "src": ("dram", [2 * K, ROWS, W], "float32"),
    "lp": ("dram", [ROWS, B], "float32"),
    "lc": ("dram", [K, ROWS, W], "float32"),
}
SEMAPHORES = (["sent", "pa", "yc", "ac", "ldp"]
              + ["ld%d_%d" % (j, k) for j in range(2) for k in range(K)]
              + ["fa%d" % k for k in range(K)] + ["ca%d" % k for k in range(K)])


def _bits(mask):
    return [1 << b for b in range(mask.bit_length()) if (mask >> b) & 1]


def _split(mask, parts):
    bits = _bits(mask)
    n = len(bits) // parts
    return [sum(bits[i * n:(i + 1) * n]) for i in range(parts)]


def _folder(topo, cores, src_chip, d):
    dc = cores[d]
    cand = [c for c in range(topo.CHIPS * topo.CORES_PER_CHIP)
            if topo.chip(c) == src_chip and topo.die(c) == topo.die(dc) and topo.may_write(c, dc)]
    free = [c for c in cand if c not in cores]
    return (free or cand)[0]


def rank_program(g, core, T, topo):
    cores = list(T.cores)
    rank = T.rank_of(core)
    chip = topo.chip(core)
    here = [r for r, c in enumerate(cores) if topo.chip(c) == chip]
    if not here:
        return
    far = [d for d in range(N) if d not in here]
    folder = {d: _folder(topo, cores, chip, d) for d in far}
    sem = T.sem

    def dst_id(c):
        rid, pid, _ = topo.addr(c)
        return DstId(rid=rid, pnc=pid)

    if rank is None:
        mine = [d for d in far if folder[d] == core]
        if not mine:
            return
        d = mine[0]
        arrive = sum(len(_bits(_split(topo.mask(cores[r], core), len(far))[0])) for r in here)
        m = topo.mask(core, cores[d])
        for k in range(K):
            g.wait_ge(sem["fa%d" % k], arrive)
            g.remote_dma_fused(
                [RemoteDMATransfer(dst_ids=[dst_id(cores[d])], dma_engine_mask=m, remote_sem=sem["ca%d" % k],
                                   srcs=[T.src[i * K + k] for i in range(len(here))], dsts=[T.lc[k]], alu_op=1)],
                local_sem=sem.sent)
        g.wait_ge(sem.sent, K * len(_bits(m)))
        return

    pos = here.index(rank)
    partner = [r for r in here if r != rank][0]
    queues = [g.sync, g.scalar]
    for k in range(K):
        for j, d in enumerate(far):
            queues[j].dma_start(T.st[j * K + k], T.x[k * RK:(k + 1) * RK, d * B:(d + 1) * B]).then_inc(
                sem["ld%d_%d" % (j, k)], 16)
    g.sync.dma_start(T.sp[:], T.x[:, partner * B:(partner + 1) * B]).then_inc(sem.ldp, 16)
    g.scalar.dma_start(T.y[:], T.x[:, rank * B:(rank + 1) * B]).then_inc(sem.yc, 16)

    sent = 0
    for k in range(K):
        trs = []
        for j, d in enumerate(far):
            g.wait_ge(sem["ld%d_%d" % (j, k)], 16)
            m = _split(topo.mask(core, folder[d]), len(far))[j]
            trs.append(RemoteDMATransfer(dst_ids=[dst_id(folder[d])], dma_engine_mask=m, remote_sem=sem["fa%d" % k],
                                         src=T.st[j * K + k], dst=T.src[pos * K + k]))
            sent += len(_bits(m))
        g.remote_dma_fused(trs, local_sem=sem.sent)
    pc = cores[partner]
    rid, pid, _ = topo.addr(pc)
    m = topo.mask(core, pc)
    g.wait_ge(sem.ldp, 16)
    g.remote_dma(out_ap=T.lp[:], in_ap=T.sp[:], remote_sem=sem.pa, local_sem=sem.sent, pid=pid, routing_id=rid,
                 dma_engine_mask=m)
    sent += len(_bits(m))
    g.wait_ge(sem.yc, 16)
    g.wait_ge(sem.pa, len(_bits(topo.mask(pc, core))))
    g.dma_start(T.y[:], T.lp[:], accum_op=AluOpType.add, max_dma_last_dim=8192).then_inc(sem.ac, 16)
    g.wait_ge(sem.ac, 16)
    for k in range(K):
        g.wait_ge(sem["ca%d" % k], len(_bits(topo.mask(cores[far[0]], core))))
        g.dma_start(T.y[k * RK:(k + 1) * RK, :], T.lc[k], accum_op=AluOpType.add, max_dma_last_dim=8192).then_inc(
            sem.ac, 16)
    g.wait_ge(sem.ac, 16 * (K + 1))
    g.wait_ge(sem.sent, sent)
